import numpy as np
import ml_dtypes


def mxq(x, axis, fmt="e4m3"):
    dtype, down = {"e4m3": (ml_dtypes.float8_e4m3fn, 7), "e5m2": (ml_dtypes.float8_e5m2, 14)}[fmt]
    v = np.moveaxis(np.asarray(x, np.float32).astype(ml_dtypes.bfloat16).astype(np.float64), axis, -1)
    blocks = v.reshape(v.shape[:-1] + (-1, 32))
    amax = np.abs(blocks).max(-1, keepdims=True)
    byte = np.maximum(np.where(amax > 0, np.frexp(amax)[1] - 1 + 127, 0) - down, 1)
    scale = np.exp2(byte - 127.0)
    codes = (blocks / scale).astype(np.float32).astype(dtype).astype(np.float64)
    return np.moveaxis((codes * scale).reshape(v.shape), -1, axis)


WIDE = False


def mx_kscale(k):
    if not WIDE:
        return np.ones(k)
    levels = np.array([10, -10, 5, -5, 0])
    if k % 512:
        return np.exp2(np.random.permutation(np.resize(levels, k // 32))).repeat(32)
    a = np.empty((k // 512, 16))
    for p in range(k // 512):
        a[p, :8] = np.random.permutation(np.resize(levels, 8))
        for g in range(8):
            far = levels[np.abs(levels - a[p, g]) >= 10]
            a[p, g + 8] = far[np.random.randint(len(far))]
    return np.exp2(a.ravel()).repeat(32)


def f64(x):
    return np.asarray(x).astype(np.float64)


def striped(idx):
    return np.tile(np.asarray(idx).reshape(-1, 16).T, (8, 1)).astype(np.uint16)


def unstriped(offs):
    return offs[:16].T.reshape(-1).astype(np.int64)


E2M1 = np.array([0.0, 0.5, 1.0, 1.5, 2.0, 3.0, 4.0, 6.0, -0.0, -0.5, -1.0, -1.5, -2.0, -3.0, -4.0, -6.0])


def pack_weight(w, fmt):
    k, n = w.shape
    w = f64(np.asarray(w, np.float32).astype(ml_dtypes.bfloat16)).reshape(k // 32, 32, n)
    amax = np.abs(w).max(1)
    if fmt == "e4m3":
        byte = np.frexp(amax)[1] - 1 + 127 - 7
    else:
        mant, ex = np.frexp(amax / 6.0)
        byte = np.where(mant > 0.5, ex, ex - 1) + 127
    byte = np.clip(np.where(amax > 0, byte, 1), 1, 254)
    scaled = (w * np.exp2(127.0 - byte)[:, None, :]).reshape(k, n).astype(np.float32)
    by_word = np.ascontiguousarray(scaled.reshape(k // 512, 128, 4, n).transpose(0, 1, 3, 2))
    if fmt == "e4m3":
        words = by_word.astype(ml_dtypes.float8_e4m3fn).view(np.uint8)
    else:
        c = by_word.astype(ml_dtypes.float4_e2m1fn).view(np.uint8) & 0xF
        words = (c[..., 0::2] | (c[..., 1::2] << 4)).reshape(k // 512, 128, 2 * n)
    return np.ascontiguousarray(words), np.ascontiguousarray(byte.astype(np.uint8).reshape(k // 512, 16, n))


def unpack_weight(words, scales, fmt):
    g, _, n = scales.shape
    words = np.ascontiguousarray(words).reshape(g, 128, n, -1)
    if fmt == "e4m3":
        vals = words.view(ml_dtypes.float8_e4m3fn).astype(np.float64)
    else:
        nib = np.empty((g, 128, n, 4), np.uint8)
        nib[..., 0::2] = words & 0xF
        nib[..., 1::2] = words >> 4
        vals = E2M1[nib]
    vals = vals * np.repeat(np.exp2(scales.astype(np.float64) - 127.0), 8, axis=1)[..., None]
    return vals.transpose(0, 1, 3, 2).reshape(g * 512, n)


def sigmoid(v):
    return 1.0 / (1.0 + np.exp(-v))


D, E, T, I, Q = 512, 512, 2048, 512, 128


def setup_inputs():
    n = np.random.standard_normal
    idx = np.random.permutation(T)[:I]
    fd = mx_kscale(D)
    fe = mx_kscale(E)
    keysp = pack_weight(n((D, T)) / fd[:, None], "e4m3")
    valsp = pack_weight(n((E, T)) / fe[:, None], "e4m3")
    return {
        "query": (n((D, Q)) * 0.5 / np.sqrt(D) * fd[:, None]).astype(np.float32),
        "query2": (n((D, Q)) * 0.8 / np.sqrt(D) * fd[:, None]).astype(np.float32),
        "keys_words": keysp[0],
        "keys_scales": keysp[1],
        "gout": (n((E, Q)) * 1 / np.sqrt(E) * fe[:, None]).astype(np.float32),
        "vals_words": valsp[0],
        "vals_scales": valsp[1],
        "size": (np.random.uniform(0.5, 2.0, (1, I))).astype(np.float32),
        "dquery2": (n((D, Q)) * 1.0 / np.sqrt(D) * fd[:, None]).astype(np.float32),
        "base": (0.5 * n((Q, T))).astype(np.float32),
        "offs": striped(idx),
    }


def reference(query, query2, keys_words, keys_scales, gout, vals_words, vals_scales, size, dquery2, base, offs):
    idx = unstriped(offs)
    keysu = unpack_weight(keys_words, keys_scales, "e4m3")
    valsu = unpack_weight(vals_words, vals_scales, "e4m3")
    queryq = mxq(f64(query), 0, "e4m3")
    keysidxg = keysu[:, idx]
    a = queryq.T @ keysidxg
    query2q = mxq(f64(query2), 0, "e4m3")
    b = query2q.T @ keysidxg
    dquery2q = mxq(f64(dquery2), 0, "e4m3")
    tb = dquery2q.T @ keysidxg
    r = np.exp(a - np.max(a, axis=1, keepdims=True))
    gt = sigmoid(b)
    p = r * gt
    z = np.sum(p, axis=1, keepdims=True)
    goutq = mxq(f64(gout), 0, "e4m3")
    valsidxg = valsu[:, idx]
    c0 = goutq.T @ valsidxg
    dz = np.sum(c0 * p * f64(size) / np.square(z) * (-1.0), axis=1, keepdims=True)
    dp = c0 / z * f64(size) + dz
    dgt = dp * r
    tgt = tb * gt * (1.0 - gt)
    tp = tgt * r
    tz = np.sum(tp, axis=1, keepdims=True)
    tdz = np.sum((tp * f64(size) * c0 - tz * z * 2.0 * c0 * p * f64(size) / np.square(z)) / np.square(z) * (-1.0), axis=1, keepdims=True)
    tdp = tz * c0 / np.square(z) * (-1.0) * f64(size) + tdz
    tdgt = tdp * r
    tdb = (tdgt * gt + tgt * dgt) * (1.0 - gt) + tgt * (-1.0) * dgt * gt
    gs = tdb * 512.0
    gf = np.zeros((Q, T))
    gf[:, idx] = gs
    y = f64(base) + gf
    return y

@@ -1,0 +1,164 @@
+from contextlib import ExitStack
+
+import concourse.mybir as mybir
+from concourse.masks import make_identity
+
+F32 = mybir.dt.float32
+BF16 = mybir.dt.bfloat16
+I32 = mybir.dt.int32
+U32 = mybir.dt.uint32
+U16 = mybir.dt.uint16
+U8 = mybir.dt.uint8
+FP8X4 = mybir.dt.float8_e4m3fn_x4
+ALU = mybir.AluOpType
+ACT = mybir.ActivationFunctionType
+AX = mybir.AxisListType
+
+P = 128
+PACK = 4
+T, SLOTS, Q = 2048, 512, 128
+FLOPS = 4 * 2 * 512 * Q * SLOTS
+CHUNKS = (256, 512, 512, 512, 256)
+
+
+def tile_attend_hvgatedexp_b_s_kernel(tc, query, query2, keys_words, keys_scales, gout, vals_words, vals_scales,
+                                       size, dquery2, base, offs, out):
+    nc = tc.nc
+    with ExitStack() as ctx:
+        sb = ctx.enter_context(tc.tile_pool(name="sb", bufs=1))
+        ps = ctx.enter_context(tc.psum_pool(name="ps", bufs=1))
+
+        def f32(name, width=SLOTS):
+            return sb.tile([P, width], F32, name=name, align_bytes=64)
+
+        offsets = sb.tile([P, SLOTS // 16], U16, name="offsets")
+        nc.sync.dma_start(offsets[:], offs)
+
+        def load_scales(name, src):
+            plane = sb.tile([P, T], U8, name=name, align_bytes=64)
+            nc.vector.memset(plane[:].bitcast(I32), 0)
+            for quad in range(4):
+                nc.sync.dma_start(plane[32 * quad : 32 * quad + 4, :].bitcast(I32),
+                                  src[0, 4 * quad : 4 * quad + 4, :].bitcast(I32))
+            return plane
+
+        def load_words(name, src):
+            words = sb.tile([P, T], U32, name=name, align_bytes=64)
+            nc.sync.dma_start(words[:].bitcast(I32), src[0].rearrange("p n t -> p (n t)").bitcast(I32))
+            return words
+
+        def load_rows(name, src):
+            raw = sb.tile([P, PACK, Q], F32, name=name)
+            nc.sync.dma_start(raw[:], src.rearrange("(p j) q -> p j q", j=PACK))
+            return raw
+
+        key_plane = load_scales("key_plane", keys_scales)
+        key_words = load_words("key_words", keys_words)
+        q2_raw = load_rows("q2_raw", query2)
+        q_raw = load_rows("q_raw", query)
+        val_plane = load_scales("val_plane", vals_scales)
+        val_words = load_words("val_words", vals_words)
+        g_raw = load_rows("g_raw", gout)
+        dq_raw = load_rows("dq_raw", dquery2)
+        size_cols = sb.tile([P, PACK], F32, name="size_cols")
+        nc.sync.dma_start(size_cols[:], size[0].rearrange("(p j) -> p j", j=PACK))
+        base_sb = f32("base_sb", T)
+        nc.sync.dma_start(base_sb[:], base)
+
+        placed = f32("placed", T)
+        nc.vector.memset(placed[:], 0.0)
+        ident = sb.tile([P, P], F32, name="ident")
+        make_identity(nc, ident[:])
+
+        def interleave(name, raw):
+            grouped = sb.tile([P, Q, PACK], BF16, name=name, align_bytes=64)
+            nc.scalar.copy(grouped[:], raw[:].rearrange("p j q -> p q j"))
+            return grouped
+
+        def quantise(name, grouped):
+            codes = sb.tile([P, Q], U32, name=name + "_codes", align_bytes=64)
+            scales = sb.tile([P, Q], U8, name=name + "_scales", align_bytes=64)
+            nc.vector.quantize_mx(codes[:].bitcast(FP8X4), scales[:], grouped[:].rearrange("p q j -> p (q j)"))
+            return codes, scales
+
+        def gather(name, window, dtype):
+            picked = sb.tile([P, SLOTS], dtype, name=name, align_bytes=64)
+            nc.vector.tensor_copy(picked[:], window[:].indirect(offsets[:]))
+            return picked
+
+        def product(name, rows, words, scales):
+            bank = ps.tile([P, SLOTS], F32, name=name)
+            nc.tensor.matmul_mx(bank[:], lhsT=rows[0][:].bitcast(FP8X4), lhsT_scale=rows[1][:],
+                                rhs=words[:].bitcast(FP8X4), rhs_scale=scales[:], start=True, stop=True)
+            return bank
+
+        q2_g = interleave("q2_g", q2_raw)
+        q_g = interleave("q_g", q_raw)
+        key_sc = gather("key_sc", key_plane, U8)
+        key_w = gather("key_w", key_words, U32)
+        q2_q = quantise("q2", q2_g)
+        q_q = quantise("q", q_g)
+        b = product("b", q2_q, key_w, key_sc)
+        a = product("a", q_q, key_w, key_sc)
+        gate = f32("gate")
+        nc.scalar.activation(gate[:], b[:], ACT.Sigmoid)
+        neg_max = f32("neg_max", 1)
+        nc.vector.tensor_reduce(neg_max[:], a[:], AX.X, ALU.max, negate=True)
+        r = f32("r")
+        nc.scalar.activation(r[:], a[:], ACT.Exp, bias=neg_max[:])
+
+        val_sc = gather("val_sc", val_plane, U8)
+        val_w = gather("val_w", val_words, U32)
+        g_g = interleave("g_g", g_raw)
+        dq_g = interleave("dq_g", dq_raw)
+        g_q = quantise("g", g_g)
+        dq_q = quantise("dq", dq_g)
+        c0 = product("c0", g_q, val_w, val_sc)
+        tb = product("tb", dq_q, key_w, key_sc)
+
+        size_bank = ps.tile([P, PACK, P], F32, name="size_bank")
+        for j in range(PACK):
+            nc.tensor.transpose(size_bank[:, j, :], size_cols[:, j : j + 1].to_broadcast([P, P]), ident[:])
+        size_rows = sb.tile([P, P, PACK], F32, name="size_rows")
+        nc.scalar.copy(size_rows[:], size_bank[:].rearrange("p j n -> p n j"))
+
+        w = f32("w")
+        nc.vector.scalar_tensor_tensor(w[:], gate[:], 0.5, tb[:], ALU.subtract, ALU.mult)
+        p = f32("p")
+        z = f32("z", 1)
+        nc.vector.scalar_tensor_tensor(p[:], r[:], 1.0, gate[:], ALU.mult, ALU.mult, accum_out=z[:])
+        c = f32("c")
+        nc.vector.tensor_tensor(c[:], c0[:], size_rows[:].rearrange("p n j -> p (n j)"), ALU.mult)
+        rz = f32("rz", 1)
+        nc.vector.reciprocal(rz[:], z[:])
+        half_rz = f32("half_rz", 1)
+        nc.scalar.mul(half_rz[:], rz[:], 0.5)
+        gain = f32("gain", 1)
+        nc.scalar.mul(gain[:], rz[:], -1024.0)
+        nu = f32("nu")
+        nc.vector.scalar_tensor_tensor(nu[:], gate[:], 1.0, p[:], ALU.subtract, ALU.mult)
+        pc = f32("pc")
+        cbar = f32("cbar", 1)
+        nc.vector.scalar_tensor_tensor(pc[:], p[:], rz[:], c[:], ALU.mult, ALU.mult, accum_out=cbar[:])
+        dev = f32("dev")
+        nc.scalar.activation(dev[:], c[:], ACT.Identity, bias=cbar[:], scale=-1.0)
+        tp = f32("tp")
+        tau = f32("tau", 1)
+        nc.vector.scalar_tensor_tensor(tp[:], nu[:], half_rz[:], tb[:], ALU.mult, ALU.mult, accum_out=tau[:])
+        td = f32("td")
+        beta = f32("beta", 1)
+        nc.vector.scalar_tensor_tensor(td[:], c[:], cbar[:], tp[:], ALU.subtract, ALU.mult, accum_out=beta[:])
+        y1 = f32("y1")
+        nc.vector.scalar_tensor_tensor(y1[:], w[:], tau[:], dev[:], ALU.subtract, ALU.mult)
+        y2 = f32("y2")
+        nc.vector.tensor_scalar(y2[:], y1[:], beta[:], gain[:], ALU.add, ALU.mult)
+        nc.vector.tensor_tensor(placed[:].indirect(offsets[:]), nu[:], y2[:], ALU.mult)
+
+        start = 0
+        for n, width in enumerate(CHUNKS):
+            cols = slice(start, start + width)
+            total = f32("total%d" % n, width)
+            nc.vector.tensor_tensor(total[:], placed[:, cols], base_sb[:, cols], ALU.add)
+            queue = nc.sync if n % 2 == 0 else nc.scalar
+            queue.dma_start(out[:, cols], total[:])
+            start = start + width

@@ -18,6 +18,8 @@ P = 128
 PACK = 4
 T, SLOTS, Q = 2048, 512, 128
 FLOPS = 4 * 2 * 512 * Q * SLOTS
+BLOCKS = SLOTS // P
+HALF = SLOTS // 2
 CHUNKS = (256, 512, 512, 512, 256)
 
 
@@ -34,34 +36,42 @@ def tile_attend_hvgatedexp_b_s_kernel(tc, query, query2, keys_words, keys_scales
         offsets = sb.tile([P, SLOTS // 16], U16, name="offsets")
         nc.sync.dma_start(offsets[:], offs)
 
-        def load_scales(name, src):
-            plane = sb.tile([P, T], U8, name=name, align_bytes=64)
-            nc.vector.memset(plane[:].bitcast(I32), 0)
+        def zeroed_plane(name, engine):
+            plane = sb.tile([P, T], U8, name=name, tag=name, align_bytes=64)
+            engine.memset(plane[:].bitcast(I32), 0)
+            return plane
+
+        def load_scales(plane, src):
             for quad in range(4):
                 nc.sync.dma_start(plane[32 * quad : 32 * quad + 4, :].bitcast(I32),
                                   src[0, 4 * quad : 4 * quad + 4, :].bitcast(I32))
-            return plane
 
         def load_words(name, src):
-            words = sb.tile([P, T], U32, name=name, align_bytes=64)
+            words = sb.tile([P, T], U32, name=name, tag=name, align_bytes=64)
             nc.sync.dma_start(words[:].bitcast(I32), src[0].rearrange("p n t -> p (n t)").bitcast(I32))
             return words
 
         def load_rows(name, src):
-            raw = sb.tile([P, PACK, Q], F32, name=name)
+            raw = sb.tile([P, PACK, Q], F32, name=name, tag=name, align_bytes=64)
             nc.sync.dma_start(raw[:], src.rearrange("(p j) q -> p j q", j=PACK))
             return raw
 
-        key_plane = load_scales("key_plane", keys_scales)
-        key_words = load_words("key_words", keys_words)
+        key_plane = zeroed_plane("key_plane", nc.gpsimd)
+        val_plane = zeroed_plane("val_plane", nc.vector)
+        warm = f32("warm", 2)
+        nc.vector.memset(warm[:, 0:1], 0.0)
+        nc.scalar.activation(warm[:, 1:2], warm[:, 0:1], ACT.Sigmoid)
         q2_raw = load_rows("q2_raw", query2)
         q_raw = load_rows("q_raw", query)
-        val_plane = load_scales("val_plane", vals_scales)
-        val_words = load_words("val_words", vals_words)
+        load_scales(key_plane, keys_scales)
+        key_words = load_words("key_words", keys_words)
         g_raw = load_rows("g_raw", gout)
         dq_raw = load_rows("dq_raw", dquery2)
-        size_cols = sb.tile([P, PACK], F32, name="size_cols")
-        nc.sync.dma_start(size_cols[:], size[0].rearrange("(p j) -> p j", j=PACK))
+        load_scales(val_plane, vals_scales)
+        val_words = load_words("val_words", vals_words)
+        size_cols = f32("size_cols", BLOCKS)
+        with nc.allow_non_contiguous_dma(reason="one weight a partition for each block of slots"):
+            nc.sync.dma_start(size_cols[:], size[0].rearrange("(j p) -> p j", p=P))
         base_sb = f32("base_sb", T)
         nc.sync.dma_start(base_sb[:], base)
 
@@ -71,7 +81,7 @@ def tile_attend_hvgatedexp_b_s_kernel(tc, query, query2, keys_words, keys_scales
         make_identity(nc, ident[:])
 
         def interleave(name, raw):
-            grouped = sb.tile([P, Q, PACK], BF16, name=name, align_bytes=64)
+            grouped = sb.tile([P, Q, PACK], BF16, name=name, tag=name, align_bytes=64)
             nc.scalar.copy(grouped[:], raw[:].rearrange("p j q -> p q j"))
             return grouped
 
@@ -92,43 +102,51 @@ def tile_attend_hvgatedexp_b_s_kernel(tc, query, query2, keys_words, keys_scales
                                 rhs=words[:].bitcast(FP8X4), rhs_scale=scales[:], start=True, stop=True)
             return bank
 
-        q2_g = interleave("q2_g", q2_raw)
-        q_g = interleave("q_g", q_raw)
+        q2_q = quantise("q2", interleave("q2_g", q2_raw))
+        q_q = quantise("q", interleave("q_g", q_raw))
         key_sc = gather("key_sc", key_plane, U8)
-        key_w = gather("key_w", key_words, U32)
-        q2_q = quantise("q2", q2_g)
-        q_q = quantise("q", q_g)
-        b = product("b", q2_q, key_w, key_sc)
-        a = product("a", q_q, key_w, key_sc)
-        gate = f32("gate")
-        nc.scalar.activation(gate[:], b[:], ACT.Sigmoid)
-        neg_max = f32("neg_max", 1)
-        nc.vector.tensor_reduce(neg_max[:], a[:], AX.X, ALU.max, negate=True)
-        r = f32("r")
-        nc.scalar.activation(r[:], a[:], ACT.Exp, bias=neg_max[:])
-
-        val_sc = gather("val_sc", val_plane, U8)
-        val_w = gather("val_w", val_words, U32)
         g_g = interleave("g_g", g_raw)
         dq_g = interleave("dq_g", dq_raw)
+
+        key_w = sb.tile([P, SLOTS], U32, name="key_w", tag="key_plane", align_bytes=64)
+        gate = sb.tile([P, SLOTS], F32, name="gate", tag="dq_raw", align_bytes=64)
+        for h in range(2):
+            half = slice(h * HALF, (h + 1) * HALF)
+            nc.vector.tensor_copy(key_w[:, half], key_words[:].indirect(offsets[:, h * HALF // 16 : (h + 1) * HALF // 16]))
+            b = ps.tile([P, HALF], F32, name="b%d" % h)
+            nc.tensor.matmul_mx(b[:], lhsT=q2_q[0][:].bitcast(FP8X4), lhsT_scale=q2_q[1][:],
+                                rhs=key_w[:, half].bitcast(FP8X4), rhs_scale=key_sc[:, half], start=True, stop=True)
+            nc.scalar.activation(gate[:, half], b[:], ACT.Sigmoid)
+        r = f32("r")
+        nc.scalar.activation(r[:, 0:1], gate[:, SLOTS - 1 : SLOTS], ACT.Exp)
+        a = product("a", q_q, key_w, key_sc)
         g_q = quantise("g", g_g)
         dq_q = quantise("dq", dq_g)
-        c0 = product("c0", g_q, val_w, val_sc)
         tb = product("tb", dq_q, key_w, key_sc)
+        val_sc = gather("val_sc", val_plane, U8)
+        neg_max = sb.tile([P, 1], F32, name="neg_max", tag="val_plane", align_bytes=64)
+        nc.vector.tensor_reduce(neg_max[:], a[:], AX.X, ALU.max, negate=True)
+        nc.scalar.activation(r[:], a[:], ACT.Exp, bias=neg_max[:])
 
-        size_bank = ps.tile([P, PACK, P], F32, name="size_bank")
-        for j in range(PACK):
-            nc.tensor.transpose(size_bank[:, j, :], size_cols[:, j : j + 1].to_broadcast([P, P]), ident[:])
-        size_rows = sb.tile([P, P, PACK], F32, name="size_rows")
-        nc.scalar.copy(size_rows[:], size_bank[:].rearrange("p j n -> p n j"))
-
-        w = f32("w")
-        nc.vector.scalar_tensor_tensor(w[:], gate[:], 0.5, tb[:], ALU.subtract, ALU.mult)
-        p = f32("p")
+        val_w = gather("val_w", val_words, U32)
+        pair = sb.tile([P, 2 * SLOTS], F32, name="pair", tag="val_words", align_bytes=64)
+        w, p = pair[:, 0:SLOTS], pair[:, SLOTS : 2 * SLOTS]
+        nc.vector.scalar_tensor_tensor(w, gate[:], 0.5, tb[:], ALU.subtract, ALU.mult)
         z = f32("z", 1)
-        nc.vector.scalar_tensor_tensor(p[:], r[:], 1.0, gate[:], ALU.mult, ALU.mult, accum_out=z[:])
-        c = f32("c")
-        nc.vector.tensor_tensor(c[:], c0[:], size_rows[:].rearrange("p n j -> p (n j)"), ALU.mult)
+        nc.vector.scalar_tensor_tensor(p, r[:], 1.0, gate[:], ALU.mult, ALU.mult, accum_out=z[:])
+        c0_t = ps.tile([P, BLOCKS, Q], F32, name="c0_t")
+        for j in range(BLOCKS):
+            block = slice(j * P, (j + 1) * P)
+            nc.tensor.matmul_mx(c0_t[:, j, :], lhsT=val_w[:, block].bitcast(FP8X4), lhsT_scale=val_sc[:, block],
+                                rhs=g_q[0][:].bitcast(FP8X4), rhs_scale=g_q[1][:], start=True, stop=True)
+        c_t = sb.tile([P, BLOCKS, Q], F32, name="c_t")
+        c = ps.tile([P, SLOTS], F32, name="c")
+        for j in range(BLOCKS):
+            nc.scalar.mul(c_t[:, j, :], c0_t[:, j, :], size_cols[:, j : j + 1])
+            nc.tensor.transpose(c[:, j * P : (j + 1) * P], c_t[:, j, :], ident[:])
+        c_again = ps.tile([P, SLOTS], F32, name="c_again")
+        for j in range(BLOCKS):
+            nc.tensor.transpose(c_again[:, j * P : (j + 1) * P], c_t[:, j, :], ident[:])
         rz = f32("rz", 1)
         nc.vector.reciprocal(rz[:], z[:])
         half_rz = f32("half_rz", 1)
@@ -136,20 +154,20 @@ def tile_attend_hvgatedexp_b_s_kernel(tc, query, query2, keys_words, keys_scales
         gain = f32("gain", 1)
         nc.scalar.mul(gain[:], rz[:], -1024.0)
         nu = f32("nu")
-        nc.vector.scalar_tensor_tensor(nu[:], gate[:], 1.0, p[:], ALU.subtract, ALU.mult)
-        pc = f32("pc")
-        cbar = f32("cbar", 1)
-        nc.vector.scalar_tensor_tensor(pc[:], p[:], rz[:], c[:], ALU.mult, ALU.mult, accum_out=cbar[:])
-        dev = f32("dev")
-        nc.scalar.activation(dev[:], c[:], ACT.Identity, bias=cbar[:], scale=-1.0)
+        nc.vector.scalar_tensor_tensor(nu[:], gate[:], 1.0, p, ALU.subtract, ALU.mult)
         tp = f32("tp")
         tau = f32("tau", 1)
         nc.vector.scalar_tensor_tensor(tp[:], nu[:], half_rz[:], tb[:], ALU.mult, ALU.mult, accum_out=tau[:])
+        pc = f32("pc")
+        cbar = f32("cbar", 1)
+        nc.vector.scalar_tensor_tensor(pc[:], c[:], rz[:], p, ALU.mult, ALU.mult, accum_out=cbar[:])
+        dev = f32("dev")
+        nc.scalar.activation(dev[:], c_again[:], ACT.Identity, bias=cbar[:], scale=-1.0)
         td = f32("td")
         beta = f32("beta", 1)
         nc.vector.scalar_tensor_tensor(td[:], c[:], cbar[:], tp[:], ALU.subtract, ALU.mult, accum_out=beta[:])
         y1 = f32("y1")
-        nc.vector.scalar_tensor_tensor(y1[:], w[:], tau[:], dev[:], ALU.subtract, ALU.mult)
+        nc.vector.scalar_tensor_tensor(y1[:], w, tau[:], dev[:], ALU.subtract, ALU.mult)
         y2 = f32("y2")
         nc.vector.tensor_scalar(y2[:], y1[:], beta[:], gain[:], ALU.add, ALU.mult)
         nc.vector.tensor_tensor(placed[:].indirect(offsets[:]), nu[:], y2[:], ALU.mult)

@@ -75,6 +75,9 @@ def tile_attend_hvgatedexp_b_s_kernel(tc, query, query2, keys_words, keys_scales
         base_sb = f32("base_sb", T)
         nc.sync.dma_start(base_sb[:], base)
 
+        factors = f32("factors", 2)
+        nc.vector.memset(factors[:, 0:1], 0.5)
+        nc.vector.memset(factors[:, 1:2], -1024.0)
         placed = f32("placed", T)
         nc.vector.memset(placed[:], 0.0)
         ident = sb.tile([P, P], F32, name="ident")
@@ -113,7 +116,7 @@ def tile_attend_hvgatedexp_b_s_kernel(tc, query, query2, keys_words, keys_scales
         for h in range(2):
             half = slice(h * HALF, (h + 1) * HALF)
             nc.vector.tensor_copy(key_w[:, half], key_words[:].indirect(offsets[:, h * HALF // 16 : (h + 1) * HALF // 16]))
-            b = ps.tile([P, HALF], F32, name="b%d" % h)
+            b = ps.tile([P, HALF], F32, name="b%d" % h, tag="b%d" % h)
             nc.tensor.matmul_mx(b[:], lhsT=q2_q[0][:].bitcast(FP8X4), lhsT_scale=q2_q[1][:],
                                 rhs=key_w[:, half].bitcast(FP8X4), rhs_scale=key_sc[:, half], start=True, stop=True)
             nc.scalar.activation(gate[:, half], b[:], ACT.Sigmoid)
@@ -134,42 +137,41 @@ def tile_attend_hvgatedexp_b_s_kernel(tc, query, query2, keys_words, keys_scales
         nc.vector.scalar_tensor_tensor(w, gate[:], 0.5, tb[:], ALU.subtract, ALU.mult)
         z = f32("z", 1)
         nc.vector.scalar_tensor_tensor(p, r[:], 1.0, gate[:], ALU.mult, ALU.mult, accum_out=z[:])
-        c0_t = ps.tile([P, BLOCKS, Q], F32, name="c0_t")
+        c0_t = [ps.tile([P, 2, Q], F32, name="c0_t%d" % h, tag="b%d" % h) for h in range(2)]
         for j in range(BLOCKS):
             block = slice(j * P, (j + 1) * P)
-            nc.tensor.matmul_mx(c0_t[:, j, :], lhsT=val_w[:, block].bitcast(FP8X4), lhsT_scale=val_sc[:, block],
+            nc.tensor.matmul_mx(c0_t[j // 2][:, j % 2, :], lhsT=val_w[:, block].bitcast(FP8X4), lhsT_scale=val_sc[:, block],
                                 rhs=g_q[0][:].bitcast(FP8X4), rhs_scale=g_q[1][:], start=True, stop=True)
         c_t = sb.tile([P, BLOCKS, Q], F32, name="c_t")
         c = ps.tile([P, SLOTS], F32, name="c")
         for j in range(BLOCKS):
-            nc.scalar.mul(c_t[:, j, :], c0_t[:, j, :], size_cols[:, j : j + 1])
+            nc.scalar.mul(c_t[:, j, :], c0_t[j // 2][:, j % 2, :], size_cols[:, j : j + 1])
             nc.tensor.transpose(c[:, j * P : (j + 1) * P], c_t[:, j, :], ident[:])
         c_again = ps.tile([P, SLOTS], F32, name="c_again")
         for j in range(BLOCKS):
             nc.tensor.transpose(c_again[:, j * P : (j + 1) * P], c_t[:, j, :], ident[:])
         rz = f32("rz", 1)
         nc.vector.reciprocal(rz[:], z[:])
-        half_rz = f32("half_rz", 1)
-        nc.scalar.mul(half_rz[:], rz[:], 0.5)
-        gain = f32("gain", 1)
-        nc.scalar.mul(gain[:], rz[:], -1024.0)
         nu = f32("nu")
         nc.vector.scalar_tensor_tensor(nu[:], gate[:], 1.0, p, ALU.subtract, ALU.mult)
-        tp = f32("tp")
-        tau = f32("tau", 1)
-        nc.vector.scalar_tensor_tensor(tp[:], nu[:], half_rz[:], tb[:], ALU.mult, ALU.mult, accum_out=tau[:])
+        scaled_rz = f32("scaled_rz", 2)
+        nc.vector.tensor_scalar(scaled_rz[:], factors[:], rz[:], None, ALU.mult)
+        half_rz, gain = scaled_rz[:, 0:1], scaled_rz[:, 1:2]
         pc = f32("pc")
         cbar = f32("cbar", 1)
         nc.vector.scalar_tensor_tensor(pc[:], c[:], rz[:], p, ALU.mult, ALU.mult, accum_out=cbar[:])
         dev = f32("dev")
         nc.scalar.activation(dev[:], c_again[:], ACT.Identity, bias=cbar[:], scale=-1.0)
+        tp = f32("tp")
+        tau = f32("tau", 1)
+        nc.vector.scalar_tensor_tensor(tp[:], nu[:], half_rz, tb[:], ALU.mult, ALU.mult, accum_out=tau[:])
         td = f32("td")
         beta = f32("beta", 1)
         nc.vector.scalar_tensor_tensor(td[:], c[:], cbar[:], tp[:], ALU.subtract, ALU.mult, accum_out=beta[:])
         y1 = f32("y1")
         nc.vector.scalar_tensor_tensor(y1[:], w, tau[:], dev[:], ALU.subtract, ALU.mult)
         y2 = f32("y2")
-        nc.vector.tensor_scalar(y2[:], y1[:], beta[:], gain[:], ALU.add, ALU.mult)
+        nc.vector.tensor_scalar(y2[:], y1[:], beta[:], gain, ALU.add, ALU.mult)
         nc.vector.tensor_tensor(placed[:].indirect(offsets[:]), nu[:], y2[:], ALU.mult)
 
         start = 0

@@ -20,7 +20,7 @@ T, SLOTS, Q = 2048, 512, 128
 FLOPS = 4 * 2 * 512 * Q * SLOTS
 BLOCKS = SLOTS // P
 HALF = SLOTS // 2
-CHUNKS = (256, 512, 512, 512, 256)
+CHUNKS = (128, 384, 512, 512, 512)
 
 
 def tile_attend_hvgatedexp_b_s_kernel(tc, query, query2, keys_words, keys_scales, gout, vals_words, vals_scales,
@@ -62,22 +62,23 @@ def tile_attend_hvgatedexp_b_s_kernel(tc, query, query2, keys_words, keys_scales
         nc.vector.memset(warm[:, 0:1], 0.0)
         nc.scalar.activation(warm[:, 1:2], warm[:, 0:1], ACT.Sigmoid)
         q2_raw = load_rows("q2_raw", query2)
-        q_raw = load_rows("q_raw", query)
         load_scales(key_plane, keys_scales)
         key_words = load_words("key_words", keys_words)
+        q_raw = load_rows("q_raw", query)
         g_raw = load_rows("g_raw", gout)
-        dq_raw = load_rows("dq_raw", dquery2)
         load_scales(val_plane, vals_scales)
         val_words = load_words("val_words", vals_words)
-        size_cols = f32("size_cols", BLOCKS)
+        dq_raw = load_rows("dq_raw", dquery2)
+        size_cols = sb.tile([P, BLOCKS], F32, name="size_cols", tag="size_cols", align_bytes=64)
         with nc.allow_non_contiguous_dma(reason="one weight a partition for each block of slots"):
             nc.sync.dma_start(size_cols[:], size[0].rearrange("(j p) -> p j", p=P))
         base_sb = f32("base_sb", T)
         nc.sync.dma_start(base_sb[:], base)
 
-        factors = f32("factors", 2)
-        nc.vector.memset(factors[:, 0:1], 0.5)
-        nc.vector.memset(factors[:, 1:2], -1024.0)
+        factors = f32("factors", 3)
+        nc.vector.memset(factors[:, 0:1], 1024.0)
+        nc.vector.memset(factors[:, 1:2], -1.0)
+        nc.vector.memset(factors[:, 2:3], -0.5)
         placed = f32("placed", T)
         nc.vector.memset(placed[:], 0.0)
         ident = sb.tile([P, P], F32, name="ident")
@@ -88,14 +89,14 @@ def tile_attend_hvgatedexp_b_s_kernel(tc, query, query2, keys_words, keys_scales
             nc.scalar.copy(grouped[:], raw[:].rearrange("p j q -> p q j"))
             return grouped
 
-        def quantise(name, grouped):
-            codes = sb.tile([P, Q], U32, name=name + "_codes", align_bytes=64)
+        def quantise(name, grouped, tag):
+            codes = sb.tile([P, Q], U32, name=name + "_codes", tag=tag, align_bytes=64)
             scales = sb.tile([P, Q], U8, name=name + "_scales", align_bytes=64)
             nc.vector.quantize_mx(codes[:].bitcast(FP8X4), scales[:], grouped[:].rearrange("p q j -> p (q j)"))
             return codes, scales
 
         def gather(name, window, dtype):
-            picked = sb.tile([P, SLOTS], dtype, name=name, align_bytes=64)
+            picked = sb.tile([P, SLOTS], dtype, name=name, tag=name, align_bytes=64)
             nc.vector.tensor_copy(picked[:], window[:].indirect(offsets[:]))
             return picked
 
@@ -105,14 +106,13 @@ def tile_attend_hvgatedexp_b_s_kernel(tc, query, query2, keys_words, keys_scales
                                 rhs=words[:].bitcast(FP8X4), rhs_scale=scales[:], start=True, stop=True)
             return bank
 
-        q2_q = quantise("q2", interleave("q2_g", q2_raw))
-        q_q = quantise("q", interleave("q_g", q_raw))
+        q2_q = quantise("q2", interleave("q2_g", q2_raw), "q2_codes")
         key_sc = gather("key_sc", key_plane, U8)
+        q_g = interleave("q_g", q_raw)
         g_g = interleave("g_g", g_raw)
-        dq_g = interleave("dq_g", dq_raw)
 
         key_w = sb.tile([P, SLOTS], U32, name="key_w", tag="key_plane", align_bytes=64)
-        gate = sb.tile([P, SLOTS], F32, name="gate", tag="dq_raw", align_bytes=64)
+        gate = sb.tile([P, SLOTS], F32, name="gate", tag="g_raw", align_bytes=64)
         for h in range(2):
             half = slice(h * HALF, (h + 1) * HALF)
             nc.vector.tensor_copy(key_w[:, half], key_words[:].indirect(offsets[:, h * HALF // 16 : (h + 1) * HALF // 16]))
@@ -122,26 +122,25 @@ def tile_attend_hvgatedexp_b_s_kernel(tc, query, query2, keys_words, keys_scales
             nc.scalar.activation(gate[:, half], b[:], ACT.Sigmoid)
         r = f32("r")
         nc.scalar.activation(r[:, 0:1], gate[:, SLOTS - 1 : SLOTS], ACT.Exp)
+        q_q = quantise("q", q_g, "q_codes")
         a = product("a", q_q, key_w, key_sc)
-        g_q = quantise("g", g_g)
-        dq_q = quantise("dq", dq_g)
-        tb = product("tb", dq_q, key_w, key_sc)
+        g_q = quantise("g", g_g, "g_codes")
         val_sc = gather("val_sc", val_plane, U8)
         neg_max = sb.tile([P, 1], F32, name="neg_max", tag="val_plane", align_bytes=64)
         nc.vector.tensor_reduce(neg_max[:], a[:], AX.X, ALU.max, negate=True)
         nc.scalar.activation(r[:], a[:], ACT.Exp, bias=neg_max[:])
 
         val_w = gather("val_w", val_words, U32)
-        pair = sb.tile([P, 2 * SLOTS], F32, name="pair", tag="val_words", align_bytes=64)
-        w, p = pair[:, 0:SLOTS], pair[:, SLOTS : 2 * SLOTS]
-        nc.vector.scalar_tensor_tensor(w, gate[:], 0.5, tb[:], ALU.subtract, ALU.mult)
+        p = sb.tile([P, SLOTS], F32, name="p", tag="val_words", align_bytes=64)
         z = f32("z", 1)
-        nc.vector.scalar_tensor_tensor(p, r[:], 1.0, gate[:], ALU.mult, ALU.mult, accum_out=z[:])
+        nc.vector.scalar_tensor_tensor(p[:], r[:], 1.0, gate[:], ALU.mult, ALU.mult, accum_out=z[:])
         c0_t = [ps.tile([P, 2, Q], F32, name="c0_t%d" % h, tag="b%d" % h) for h in range(2)]
         for j in range(BLOCKS):
             block = slice(j * P, (j + 1) * P)
             nc.tensor.matmul_mx(c0_t[j // 2][:, j % 2, :], lhsT=val_w[:, block].bitcast(FP8X4), lhsT_scale=val_sc[:, block],
                                 rhs=g_q[0][:].bitcast(FP8X4), rhs_scale=g_q[1][:], start=True, stop=True)
+        dq_q = quantise("dq", interleave("val_plane", dq_raw), "val_w")
+        tb = product("tb", dq_q, key_w, key_sc)
         c_t = sb.tile([P, BLOCKS, Q], F32, name="c_t")
         c = ps.tile([P, SLOTS], F32, name="c")
         for j in range(BLOCKS):
@@ -153,26 +152,29 @@ def tile_attend_hvgatedexp_b_s_kernel(tc, query, query2, keys_words, keys_scales
         rz = f32("rz", 1)
         nc.vector.reciprocal(rz[:], z[:])
         nu = f32("nu")
-        nc.vector.scalar_tensor_tensor(nu[:], gate[:], 1.0, p, ALU.subtract, ALU.mult)
-        scaled_rz = f32("scaled_rz", 2)
+        nc.vector.scalar_tensor_tensor(nu[:], gate[:], 1.0, p[:], ALU.subtract, ALU.mult)
+        scaled_rz = f32("scaled_rz", 3)
         nc.vector.tensor_scalar(scaled_rz[:], factors[:], rz[:], None, ALU.mult)
-        half_rz, gain = scaled_rz[:, 0:1], scaled_rz[:, 1:2]
-        pc = f32("pc")
-        cbar = f32("cbar", 1)
-        nc.vector.scalar_tensor_tensor(pc[:], c[:], rz[:], p, ALU.mult, ALU.mult, accum_out=cbar[:])
-        dev = f32("dev")
-        nc.scalar.activation(dev[:], c_again[:], ACT.Identity, bias=cbar[:], scale=-1.0)
         tp = f32("tp")
         tau = f32("tau", 1)
-        nc.vector.scalar_tensor_tensor(tp[:], nu[:], half_rz, tb[:], ALU.mult, ALU.mult, accum_out=tau[:])
+        nc.vector.scalar_tensor_tensor(tp[:], nu[:], scaled_rz[:, 0:1], tb[:], ALU.mult, ALU.mult, accum_out=tau[:])
+        pc = f32("pc")
+        neg_cbar = f32("neg_cbar", 1)
+        nc.vector.scalar_tensor_tensor(pc[:], c[:], scaled_rz[:, 1:2], p[:], ALU.mult, ALU.mult, accum_out=neg_cbar[:])
+        u = sb.tile([P, SLOTS], F32, name="u", tag="size_cols", align_bytes=64)
+        nc.scalar.mul(u[:], nu[:], scaled_rz[:, 2:3])
+        shift = f32("shift", 1)
+        nc.scalar.mul(shift[:], neg_cbar[:], tau[:])
+        drift = f32("drift")
+        nc.scalar.activation(drift[:], c_again[:], ACT.Identity, bias=shift[:], scale=tau[:])
         td = f32("td")
         beta = f32("beta", 1)
-        nc.vector.scalar_tensor_tensor(td[:], c[:], cbar[:], tp[:], ALU.subtract, ALU.mult, accum_out=beta[:])
-        y1 = f32("y1")
-        nc.vector.scalar_tensor_tensor(y1[:], w, tau[:], dev[:], ALU.subtract, ALU.mult)
-        y2 = f32("y2")
-        nc.vector.tensor_scalar(y2[:], y1[:], beta[:], gain, ALU.add, ALU.mult)
-        nc.vector.tensor_tensor(placed[:].indirect(offsets[:]), nu[:], y2[:], ALU.mult)
+        nc.vector.scalar_tensor_tensor(td[:], c[:], neg_cbar[:], tp[:], ALU.add, ALU.mult, accum_out=beta[:])
+        first = f32("first")
+        nc.vector.scalar_tensor_tensor(first[:], gate[:], 0.5, td[:], ALU.subtract, ALU.mult)
+        second = f32("second")
+        nc.vector.scalar_tensor_tensor(second[:], drift[:], beta[:], u[:], ALU.add, ALU.mult)
+        nc.vector.tensor_tensor(placed[:].indirect(offsets[:]), first[:], second[:], ALU.add)
 
         start = 0
         for n, width in enumerate(CHUNKS):

@@ -46,13 +46,13 @@ def tile_attend_hvgatedexp_b_s_kernel(tc, query, query2, keys_words, keys_scales
                 nc.sync.dma_start(plane[32 * quad : 32 * quad + 4, :].bitcast(I32),
                                   src[0, 4 * quad : 4 * quad + 4, :].bitcast(I32))
 
-        def load_words(name, src):
-            words = sb.tile([P, T], U32, name=name, tag=name, align_bytes=64)
+        def load_words(name, src, tag):
+            words = sb.tile([P, T], U32, name=name, tag=tag, align_bytes=64)
             nc.sync.dma_start(words[:].bitcast(I32), src[0].rearrange("p n t -> p (n t)").bitcast(I32))
             return words
 
-        def load_rows(name, src):
-            raw = sb.tile([P, PACK, Q], F32, name=name, tag=name, align_bytes=64)
+        def load_rows(name, src, tag):
+            raw = sb.tile([P, PACK, Q], F32, name=name, tag=tag, align_bytes=64)
             nc.sync.dma_start(raw[:], src.rearrange("(p j) q -> p j q", j=PACK))
             return raw
 
@@ -61,19 +61,12 @@ def tile_attend_hvgatedexp_b_s_kernel(tc, query, query2, keys_words, keys_scales
         warm = f32("warm", 2)
         nc.vector.memset(warm[:, 0:1], 0.0)
         nc.scalar.activation(warm[:, 1:2], warm[:, 0:1], ACT.Sigmoid)
-        q2_raw = load_rows("q2_raw", query2)
+        q2_raw = load_rows("q2_raw", query2, "val_words")
         load_scales(key_plane, keys_scales)
-        key_words = load_words("key_words", keys_words)
-        q_raw = load_rows("q_raw", query)
-        g_raw = load_rows("g_raw", gout)
+        key_words = load_words("key_words", keys_words, "key_words")
+        q_raw = load_rows("q_raw", query, "q_raw")
+        g_raw = load_rows("g_raw", gout, "g_raw")
         load_scales(val_plane, vals_scales)
-        val_words = load_words("val_words", vals_words)
-        dq_raw = load_rows("dq_raw", dquery2)
-        size_cols = sb.tile([P, BLOCKS], F32, name="size_cols", tag="size_cols", align_bytes=64)
-        with nc.allow_non_contiguous_dma(reason="one weight a partition for each block of slots"):
-            nc.sync.dma_start(size_cols[:], size[0].rearrange("(j p) -> p j", p=P))
-        base_sb = f32("base_sb", T)
-        nc.sync.dma_start(base_sb[:], base)
 
         factors = f32("factors", 3)
         nc.vector.memset(factors[:, 0:1], 1024.0)
@@ -107,8 +100,13 @@ def tile_attend_hvgatedexp_b_s_kernel(tc, query, query2, keys_words, keys_scales
             return bank
 
         q2_q = quantise("q2", interleave("q2_g", q2_raw), "q2_codes")
+        val_words = load_words("val_words", vals_words, "val_words")
+        size_cols = sb.tile([P, BLOCKS], F32, name="size_cols", tag="q2_g", align_bytes=64)
+        with nc.allow_non_contiguous_dma(reason="one weight a partition for each block of slots"):
+            nc.sync.dma_start(size_cols[:], size[0].rearrange("(j p) -> p j", p=P))
         key_sc = gather("key_sc", key_plane, U8)
         q_g = interleave("q_g", q_raw)
+        dq_raw = load_rows("dq_raw", dquery2, "q_raw")
         g_g = interleave("g_g", g_raw)
 
         key_w = sb.tile([P, SLOTS], U32, name="key_w", tag="key_plane", align_bytes=64)
@@ -123,6 +121,8 @@ def tile_attend_hvgatedexp_b_s_kernel(tc, query, query2, keys_words, keys_scales
         r = f32("r")
         nc.scalar.activation(r[:, 0:1], gate[:, SLOTS - 1 : SLOTS], ACT.Exp)
         q_q = quantise("q", q_g, "q_codes")
+        base_sb = sb.tile([P, T], F32, name="base_sb", tag="q_g", align_bytes=64)
+        nc.sync.dma_start(base_sb[:], base)
         a = product("a", q_q, key_w, key_sc)
         g_q = quantise("g", g_g, "g_codes")
         val_sc = gather("val_sc", val_plane, U8)
@@ -161,7 +161,7 @@ def tile_attend_hvgatedexp_b_s_kernel(tc, query, query2, keys_words, keys_scales
         pc = f32("pc")
         neg_cbar = f32("neg_cbar", 1)
         nc.vector.scalar_tensor_tensor(pc[:], c[:], scaled_rz[:, 1:2], p[:], ALU.mult, ALU.mult, accum_out=neg_cbar[:])
-        u = sb.tile([P, SLOTS], F32, name="u", tag="size_cols", align_bytes=64)
+        u = sb.tile([P, SLOTS], F32, name="u", tag="q2_g", align_bytes=64)
         nc.scalar.mul(u[:], nu[:], scaled_rz[:, 2:3])
         shift = f32("shift", 1)
         nc.scalar.mul(shift[:], neg_cbar[:], tau[:])

from contextlib import ExitStack

import concourse.mybir as mybir
from concourse.masks import make_identity

F32 = mybir.dt.float32
BF16 = mybir.dt.bfloat16
I32 = mybir.dt.int32
U32 = mybir.dt.uint32
U16 = mybir.dt.uint16
U8 = mybir.dt.uint8
FP8X4 = mybir.dt.float8_e4m3fn_x4
ALU = mybir.AluOpType
ACT = mybir.ActivationFunctionType
AX = mybir.AxisListType

P = 128
PACK = 4
T, SLOTS, Q = 2048, 512, 128
FLOPS = 4 * 2 * 512 * Q * SLOTS
BLOCKS = SLOTS // P
HALF = SLOTS // 2
CHUNKS = (128, 384, 512, 512, 512)


def tile_attend_hvgatedexp_b_s_kernel(tc, query, query2, keys_words, keys_scales, gout, vals_words, vals_scales,
                                       size, dquery2, base, offs, out):
    nc = tc.nc
    with ExitStack() as ctx:
        sb = ctx.enter_context(tc.tile_pool(name="sb", bufs=1))
        ps = ctx.enter_context(tc.psum_pool(name="ps", bufs=1))

        def f32(name, width=SLOTS):
            return sb.tile([P, width], F32, name=name, align_bytes=64)

        offsets = sb.tile([P, SLOTS // 16], U16, name="offsets")
        nc.sync.dma_start(offsets[:], offs)

        def zeroed_plane(name, engine):
            plane = sb.tile([P, T], U8, name=name, tag=name, align_bytes=64)
            engine.memset(plane[:].bitcast(I32), 0)
            return plane

        def load_scales(plane, src):
            for quad in range(4):
                nc.sync.dma_start(plane[32 * quad : 32 * quad + 4, :].bitcast(I32),
                                  src[0, 4 * quad : 4 * quad + 4, :].bitcast(I32))

        def load_words(name, src, tag):
            words = sb.tile([P, T], U32, name=name, tag=tag, align_bytes=64)
            nc.sync.dma_start(words[:].bitcast(I32), src[0].rearrange("p n t -> p (n t)").bitcast(I32))
            return words

        def load_rows(name, src, tag):
            raw = sb.tile([P, PACK, Q], F32, name=name, tag=tag, align_bytes=64)
            nc.sync.dma_start(raw[:], src.rearrange("(p j) q -> p j q", j=PACK))
            return raw

        key_plane = zeroed_plane("key_plane", nc.gpsimd)
        val_plane = zeroed_plane("val_plane", nc.vector)
        warm = f32("warm", 2)
        nc.vector.memset(warm[:, 0:1], 0.0)
        nc.scalar.activation(warm[:, 1:2], warm[:, 0:1], ACT.Sigmoid)
        q2_raw = load_rows("q2_raw", query2, "val_words")
        load_scales(key_plane, keys_scales)
        key_words = load_words("key_words", keys_words, "key_words")
        q_raw = load_rows("q_raw", query, "q_raw")
        g_raw = load_rows("g_raw", gout, "g_raw")
        load_scales(val_plane, vals_scales)

        factors = f32("factors", 3)
        nc.vector.memset(factors[:, 0:1], 1024.0)
        nc.vector.memset(factors[:, 1:2], -1.0)
        nc.vector.memset(factors[:, 2:3], -0.5)
        placed = f32("placed", T)
        nc.vector.memset(placed[:], 0.0)
        ident = sb.tile([P, P], F32, name="ident")
        make_identity(nc, ident[:])

        def interleave(name, raw):
            grouped = sb.tile([P, Q, PACK], BF16, name=name, tag=name, align_bytes=64)
            nc.scalar.copy(grouped[:], raw[:].rearrange("p j q -> p q j"))
            return grouped

        def quantise(name, grouped, tag):
            codes = sb.tile([P, Q], U32, name=name + "_codes", tag=tag, align_bytes=64)
            scales = sb.tile([P, Q], U8, name=name + "_scales", align_bytes=64)
            nc.vector.quantize_mx(codes[:].bitcast(FP8X4), scales[:], grouped[:].rearrange("p q j -> p (q j)"))
            return codes, scales

        def gather(name, window, dtype):
            picked = sb.tile([P, SLOTS], dtype, name=name, tag=name, align_bytes=64)
            nc.vector.tensor_copy(picked[:], window[:].indirect(offsets[:]))
            return picked

        def product(name, rows, words, scales):
            bank = ps.tile([P, SLOTS], F32, name=name)
            nc.tensor.matmul_mx(bank[:], lhsT=rows[0][:].bitcast(FP8X4), lhsT_scale=rows[1][:],
                                rhs=words[:].bitcast(FP8X4), rhs_scale=scales[:], start=True, stop=True)
            return bank

        q2_q = quantise("q2", interleave("q2_g", q2_raw), "q2_codes")
        val_words = load_words("val_words", vals_words, "val_words")
        size_cols = sb.tile([P, BLOCKS], F32, name="size_cols", tag="q2_g", align_bytes=64)
        with nc.allow_non_contiguous_dma(reason="one weight a partition for each block of slots"):
            nc.sync.dma_start(size_cols[:], size[0].rearrange("(j p) -> p j", p=P))
        key_sc = gather("key_sc", key_plane, U8)
        q_g = interleave("q_g", q_raw)
        dq_raw = load_rows("dq_raw", dquery2, "q_raw")
        g_g = interleave("g_g", g_raw)

        key_w = sb.tile([P, SLOTS], U32, name="key_w", tag="key_plane", align_bytes=64)
        gate = sb.tile([P, SLOTS], F32, name="gate", tag="g_raw", align_bytes=64)
        for h in range(2):
            half = slice(h * HALF, (h + 1) * HALF)
            nc.vector.tensor_copy(key_w[:, half], key_words[:].indirect(offsets[:, h * HALF // 16 : (h + 1) * HALF // 16]))
            b = ps.tile([P, HALF], F32, name="b%d" % h, tag="b%d" % h)
            nc.tensor.matmul_mx(b[:], lhsT=q2_q[0][:].bitcast(FP8X4), lhsT_scale=q2_q[1][:],
                                rhs=key_w[:, half].bitcast(FP8X4), rhs_scale=key_sc[:, half], start=True, stop=True)
            nc.scalar.activation(gate[:, half], b[:], ACT.Sigmoid)
        r = f32("r")
        nc.scalar.activation(r[:, 0:1], gate[:, SLOTS - 1 : SLOTS], ACT.Exp)
        q_q = quantise("q", q_g, "q_codes")
        base_sb = sb.tile([P, T], F32, name="base_sb", tag="q_g", align_bytes=64)
        nc.sync.dma_start(base_sb[:], base)
        a = product("a", q_q, key_w, key_sc)
        g_q = quantise("g", g_g, "g_codes")
        val_sc = gather("val_sc", val_plane, U8)
        neg_max = sb.tile([P, 1], F32, name="neg_max", tag="val_plane", align_bytes=64)
        nc.vector.tensor_reduce(neg_max[:], a[:], AX.X, ALU.max, negate=True)
        nc.scalar.activation(r[:], a[:], ACT.Exp, bias=neg_max[:])

        val_w = gather("val_w", val_words, U32)
        p = sb.tile([P, SLOTS], F32, name="p", tag="val_words", align_bytes=64)
        z = f32("z", 1)
        nc.vector.scalar_tensor_tensor(p[:], r[:], 1.0, gate[:], ALU.mult, ALU.mult, accum_out=z[:])
        c0_t = [ps.tile([P, 2, Q], F32, name="c0_t%d" % h, tag="b%d" % h) for h in range(2)]
        for j in range(BLOCKS):
            block = slice(j * P, (j + 1) * P)
            nc.tensor.matmul_mx(c0_t[j // 2][:, j % 2, :], lhsT=val_w[:, block].bitcast(FP8X4), lhsT_scale=val_sc[:, block],
                                rhs=g_q[0][:].bitcast(FP8X4), rhs_scale=g_q[1][:], start=True, stop=True)
        dq_q = quantise("dq", interleave("val_plane", dq_raw), "val_w")
        tb = product("tb", dq_q, key_w, key_sc)
        c_t = sb.tile([P, BLOCKS, Q], F32, name="c_t")
        c = ps.tile([P, SLOTS], F32, name="c")
        for j in range(BLOCKS):
            nc.scalar.mul(c_t[:, j, :], c0_t[j // 2][:, j % 2, :], size_cols[:, j : j + 1])
            nc.tensor.transpose(c[:, j * P : (j + 1) * P], c_t[:, j, :], ident[:])
        c_again = ps.tile([P, SLOTS], F32, name="c_again")
        for j in range(BLOCKS):
            nc.tensor.transpose(c_again[:, j * P : (j + 1) * P], c_t[:, j, :], ident[:])
        rz = f32("rz", 1)
        nc.vector.reciprocal(rz[:], z[:])
        nu = f32("nu")
        nc.vector.scalar_tensor_tensor(nu[:], gate[:], 1.0, p[:], ALU.subtract, ALU.mult)
        scaled_rz = f32("scaled_rz", 3)
        nc.vector.tensor_scalar(scaled_rz[:], factors[:], rz[:], None, ALU.mult)
        tp = f32("tp")
        tau = f32("tau", 1)
        nc.vector.scalar_tensor_tensor(tp[:], nu[:], scaled_rz[:, 0:1], tb[:], ALU.mult, ALU.mult, accum_out=tau[:])
        pc = f32("pc")
        neg_cbar = f32("neg_cbar", 1)
        nc.vector.scalar_tensor_tensor(pc[:], c[:], scaled_rz[:, 1:2], p[:], ALU.mult, ALU.mult, accum_out=neg_cbar[:])
        u = sb.tile([P, SLOTS], F32, name="u", tag="q2_g", align_bytes=64)
        nc.scalar.mul(u[:], nu[:], scaled_rz[:, 2:3])
        shift = f32("shift", 1)
        nc.scalar.mul(shift[:], neg_cbar[:], tau[:])
        drift = f32("drift")
        nc.scalar.activation(drift[:], c_again[:], ACT.Identity, bias=shift[:], scale=tau[:])
        td = f32("td")
        beta = f32("beta", 1)
        nc.vector.scalar_tensor_tensor(td[:], c[:], neg_cbar[:], tp[:], ALU.add, ALU.mult, accum_out=beta[:])
        first = f32("first")
        nc.vector.scalar_tensor_tensor(first[:], gate[:], 0.5, td[:], ALU.subtract, ALU.mult)
        second = f32("second")
        nc.vector.scalar_tensor_tensor(second[:], drift[:], beta[:], u[:], ALU.add, ALU.mult)
        nc.vector.tensor_tensor(placed[:].indirect(offsets[:]), first[:], second[:], ALU.add)

        start = 0
        for n, width in enumerate(CHUNKS):
            cols = slice(start, start + width)
            total = f32("total%d" % n, width)
            nc.vector.tensor_tensor(total[:], placed[:, cols], base_sb[:, cols], ALU.add)
            queue = nc.sync if n % 2 == 0 else nc.scalar
            queue.dma_start(out[:, cols], total[:])
            start = start + width
